import numpy as np, ml_dtypes
CORES = [120,124,248,252,376,380,504,508]
N = 8
DEG, TK, TIMES = 4, 64, 3
MASK = [[0,4,6,7],[1,2,6,7],[0,2,4,7],[2,3,5,7],[2,3,4,6],[0,3,5,6],[1,4,5,6],[1,3,6,7]]
def setup_inputs(rng):
    return {"x": rng.standard_normal((N, 128, TK), dtype=np.float32).astype(ml_dtypes.bfloat16), "w": (rng.standard_normal((N, 128, DEG * 128), dtype=np.float32) / np.float32(np.sqrt(128 * DEG / 2))).astype(ml_dtypes.bfloat16)}
def setup_inputs_big(rng):
    d = setup_inputs(rng)
    for k in ("x",): d[k] = (d[k].astype(np.float32) * 1048576.0).astype(d[k].dtype)
    return d
def setup_inputs_small(rng):
    d = setup_inputs(rng)
    for k in ("x",): d[k] = (d[k].astype(np.float32) * (1 / 1048576.0)).astype(d[k].dtype)
    return d
def setup_inputs_apart(rng):
    d = setup_inputs(rng)
    f = (10.0 ** rng.permutation(np.linspace(-1.5, 1.5, N))).astype(np.float32).reshape(N, 1, 1)
    for k in ("x",): d[k] = (d[k].astype(np.float32) * f).astype(d[k].dtype)
    return d
def reference(x, w):
    X, W = x.astype(np.float64), w.astype(np.float64)
    h = list(X)
    for _ in range(TIMES):
        h = [np.maximum(sum(W[r][:, 128 * i:128 * i + 128].T @ h[j] for i, j in enumerate(MASK[r])), 0.0) for r in range(N)]
    return {"y": np.stack(h).astype(ml_dtypes.bfloat16)}

@@ -1,0 +1,175 @@
+from concourse.bass import DstId, RemoteDMATransfer
+from concourse.mybir import AluOpType
+
+N, DEG, TK, TIMES, P = 8, 4, 64, 3, 128
+ORDER = [1, 2, 3, 4, 5, 6, 7, 0]
+
+SCRATCH = {
+    "h": ("sbuf", [P, TIMES * N * TK], "bfloat16"),
+    "wo": ("sbuf", [P, DEG * P], "bfloat16"),
+    "wr": ("sbuf", [P, DEG * P], "bfloat16"),
+    "zero": ("sbuf", [P, TK], "float32"),
+    "yb": ("sbuf", [P, TK], "bfloat16"),
+    "p0": ("psum", [P, 512], "float32"),
+    "p1": ("psum", [P, 512], "float32"),
+    "p2": ("psum", [P, 512], "float32"),
+    "p3": ("psum", [P, 512], "float32"),
+    "p4": ("psum", [P, 512], "float32"),
+}
+SEMAPHORES = (["s%d%d" % (t, j) for t in range(TIMES) for j in range(N)]
+              + ["m%d" % i for i in range(5)] + ["sw", "swr", "sz", "s3", "sy", "sent"])
+
+REP = {0: 7, 7: 0, 4: 3, 3: 4}
+
+
+def _h(t, js, dests, part="all"):
+    return ("h", t, js, dests, part)
+
+
+def _w(dest, part="all"):
+    return ("w", 0, [], [dest], part)
+
+
+SENDS = {
+    0: [[_h(0, [0], [2, 7])], [_w(7)], [_h(1, [7, 0], [2, 3])], [_h(2, [7, 0], [2, 3])]],
+    1: [[_h(0, [1], [6, 7, 0])], [_h(0, [7], [2, 3])], [_h(1, [1], [6, 7, 0])], [_h(1, [6], [3])], [_h(2, [1], [6, 7])]],
+    2: [[_h(0, [2], [4, 1, 3])], [_h(0, [0], [5])], [_h(1, [2], [4, 1, 3])], [_h(2, [2], [4, 1, 3])]],
+    3: [[_h(0, [3], [5, 4, 0])], [_w(4)], [_h(1, [3], [5, 0])], [_h(2, [3], [5], "lo"), _h(2, [4], [0], "hi")]],
+    4: [[_h(0, [4], [6, 2, 7])], [_w(3, "hi")], [_h(1, [4], [6, 2, 3, 7], "lo")], [_h(1, [3], [7])],
+        [_h(2, [4], [6, 2], "lo"), _h(2, [3], [7], "hi")]],
+    5: [[_h(0, [5], [3, 6, 4])], [_h(0, [3], [7])], [_h(1, [5], [3, 6, 4])], [_h(2, [5], [3, 6])]],
+    6: [[_h(0, [6], [4, 0, 1, 5, 7])], [_h(0, [4], [0])], [_h(1, [6], [1, 0, 4, 5, 7])], [_h(1, [4], [0])],
+        [_h(2, [6], [0, 1, 4, 5, 7])]],
+    7: [[_h(0, [7], [1, 0, 4])], [_w(0)], [_h(1, [7], [1, 4])], [_h(1, [0], [5])], [_h(2, [0], [5])], [_h(2, [7], [1])]],
+}
+
+GROUPS = {
+    0: [(1, 0, [0, 6, 7, 4]), (1, 7, [1, 3, 6, 7]), (2, 0, [0, 6, 4, 7]), (2, 7, [7, 1, 6, 3]), (3, 0, [0, 7, 6, 4])],
+    1: [(1, 1, [1, 2, 6, 7]), (2, 1, [1, 6, 2, 7]), (3, 1, [1, 2, 7, 6])],
+    2: [(1, 2, [2, 0, 4, 7]), (2, 2, [2, 4, 0, 7]), (3, 2, [2, 4, 0, 7])],
+    3: [(1, 3, [3, 2, 5, 7]), (2, 3, [3, 2, 5, 7]), (2, 4, [3, 2, 4, 6]), (3, 3, [3, 2, 5, 7])],
+    4: [(1, 4, [4, 2, 3, 6]), (1, 3, [2, 3, 5, 7]), (2, 4, [4, 6, 3, 2]), (2, 3, [3, 2, 5, 7]), (3, 4, [4, 3, 2, 6])],
+    5: [(1, 5, [5, 3, 6, 0]), (2, 5, [5, 6, 3, 0]), (3, 5, [5, 0, 3, 6])],
+    6: [(1, 6, [6, 1, 4, 5]), (2, 6, [6, 1, 4, 5]), (3, 6, [6, 1, 4, 5])],
+    7: [(1, 7, [7, 6, 1, 3]), (1, 0, [7, 6, 0, 4]), (2, 0, [7, 0, 4, 6]), (2, 7, [7, 1, 6, 3]), (3, 7, [7, 1, 6, 3])],
+}
+
+
+def _col(t, j):
+    return (t * N + ORDER.index(j)) * TK
+
+
+def _bits(m):
+    return [b for b in range(m.bit_length()) if (m >> b) & 1]
+
+
+def _mask(engines):
+    return sum(1 << b for b in engines)
+
+
+def _plan(cores, topo):
+    have, calls, wcount = {}, {}, {}
+    for r in range(N):
+        have[(r, (0, r))] = ("s0%d" % r, 16)
+        for t, k, _ in GROUPS[r]:
+            if t < TIMES:
+                have[(r, (t, k))] = ("s%d%d" % (t, k), 1)
+
+    def near(a, b):
+        return topo.host(a) == topo.host(b) and topo.chip(a) == topo.chip(b)
+
+    for r in range(N):
+        me = cores[r]
+        off = 0
+        for c in cores:
+            if not near(me, c) and topo.may_write(me, c):
+                off = topo.mask(me, c)
+        calls[r] = []
+        for call in SENDS[r]:
+            now, later = [], []
+            for kind, t, js, dests, part in call:
+                for d in dests:
+                    assert topo.may_write(me, cores[d])
+                far = [d for d in dests if not near(me, cores[d])]
+                nbr = [d for d in dests if near(me, cores[d])]
+                for group in (far, nbr):
+                    if not group:
+                        continue
+                    m = topo.mask(me, cores[group[0]])
+                    eng = _bits(m & off) if group is far else _bits(m & ~off)
+                    if part == "lo":
+                        eng = eng[:len(eng) // 2]
+                    elif part == "hi":
+                        eng = eng[len(eng) // 2:]
+                    (later if (group is nbr and t == 0 and far) else now).append((kind, t, js, group, eng))
+                    for d in group:
+                        if kind == "w":
+                            wcount[d] = len(eng)
+                        for j in js:
+                            assert (d, (t, j)) not in have
+                            have[(d, (t, j))] = ("s%d%d" % (t, js[0]), len(eng))
+            calls[r].append(now)
+            if later:
+                calls[r].append(later)
+    return have, calls, wcount
+
+
+def rank_program(g, core, T, topo):
+    r = T.rank_of(core)
+    if r is None:
+        return
+    mask_table = T.tables["MASK"]
+    have, calls, wcount = _plan(T.cores, topo)
+    S = T.sem
+
+    def hs(t, js):
+        for a, b in zip(js, js[1:]):
+            assert ORDER.index(b) == ORDER.index(a) + 1
+        c0 = _col(t, js[0])
+        return T.h[:, c0:c0 + TK * len(js)]
+
+    g.sync.dma_start(hs(0, [r]), T.x[:]).then_inc(S["s0%d" % r], 16)
+    g.scalar.dma_start(T.wo[:], T.w[:]).then_inc(S.sw, 16)
+    g.vector.memset(T.zero[:], 0.0).then_inc(S.sz, 1)
+    g.vector.wait_ge(S.sz, 1)
+
+    seen = set()
+    for gi, (t, k, order) in enumerate(GROUPS[r]):
+        assert sorted(order) == sorted(mask_table[k]) and (k == r or REP[r] == k)
+        wt, wsem = (T.wo, ("sw", 16)) if k == r else (T.wr, ("swr", wcount[r]))
+        ps = T["p%d" % gi]
+        mm = None
+        for n, j in enumerate(order):
+            i = mask_table[k].index(j)
+            for sem in (wsem, have[(r, (t - 1, j))]):
+                if sem not in seen:
+                    g.tensor.wait_ge(S[sem[0]], sem[1])
+                    seen.add(sem)
+            mm = g.tensor.matmul(ps[:, 0:TK], wt[:, P * i:P * i + P], hs(t - 1, [j]), start=(n == 0), stop=(n == DEG - 1))
+        mm.then_inc(S["m%d" % gi], 1)
+        g.vector.wait_ge(S["m%d" % gi], 1)
+        out, osem = (hs(t, [k]), S["s%d%d" % (t, k)]) if t < TIMES else (T.yb[:], S.s3)
+        g.vector.tensor_tensor(out, ps[:, 0:TK], T.zero[:], AluOpType.max).then_inc(osem, 1)
+
+    seen, total = set(), 0
+    for call in calls[r]:
+        transfers = []
+        for kind, t, js, dests, eng in call:
+            for sem in ([("sw", 16)] if kind == "w" else [have[(r, (t, j))] for j in js]):
+                if sem not in seen:
+                    g.wait_ge(S[sem[0]], sem[1])
+                    seen.add(sem)
+            ids = []
+            for d in dests:
+                rid, pid = topo.addr(T.cores[d], core)
+                ids.append(DstId(rid=rid, pnc=pid))
+            src, dst, rsem = (T.wo[:], T.wr[:], S.swr) if kind == "w" else (hs(t, js), hs(t, js), S["s%d%d" % (t, js[0])])
+            transfers.append(RemoteDMATransfer(dst_ids=ids, dma_engine_mask=_mask(eng), remote_sem=rsem,
+                                               srcs=[src], dsts=[dst for _ in dests]))
+            total += len(eng)
+        g.remote_dma_fused(transfers, local_sem=S.sent)
+    g.wait_ge(S.sent, total)
+
+    g.sync.wait_ge(S.s3, 1)
+    g.sync.dma_start(T.y[:], T.yb[:]).then_inc(S.sy, 16)
+    g.sync.wait_ge(S.sy, 16)

@@ -2,12 +2,14 @@ from concourse.bass import DstId, RemoteDMATransfer
 from concourse.mybir import AluOpType
 
 N, DEG, TK, TIMES, P = 8, 4, 64, 3, 128
+HW = DEG * P // 2
 ORDER = [1, 2, 3, 4, 5, 6, 7, 0]
 
 SCRATCH = {
     "h": ("sbuf", [P, TIMES * N * TK], "bfloat16"),
     "wo": ("sbuf", [P, DEG * P], "bfloat16"),
     "wr": ("sbuf", [P, DEG * P], "bfloat16"),
+    "xd": ("dram", [P, TK], "bfloat16"),
     "zero": ("sbuf", [P, TK], "float32"),
     "yb": ("sbuf", [P, TK], "bfloat16"),
     "p0": ("psum", [P, 512], "float32"),
@@ -17,7 +19,7 @@ SCRATCH = {
     "p4": ("psum", [P, 512], "float32"),
 }
 SEMAPHORES = (["s%d%d" % (t, j) for t in range(TIMES) for j in range(N)]
-              + ["m%d" % i for i in range(5)] + ["sw", "swr", "sz", "s3", "sy", "sent"])
+              + ["m%d" % i for i in range(5)] + ["sw0", "sw1", "swr0", "swr1", "sxd", "sz", "s3", "sy", "sent"])
 
 REP = {0: 7, 7: 0, 4: 3, 3: 4}
 
@@ -26,32 +28,36 @@ def _h(t, js, dests, part="all"):
     return ("h", t, js, dests, part)
 
 
-def _w(dest, part="all"):
-    return ("w", 0, [], [dest], part)
+def _w(half, dest, part="all"):
+    return ("w", half, [], [dest], part)
 
 
 SENDS = {
-    0: [[_h(0, [0], [2, 7])], [_w(7)], [_h(1, [7, 0], [2, 3])], [_h(2, [7, 0], [2, 3])]],
-    1: [[_h(0, [1], [6, 7, 0])], [_h(0, [7], [2, 3])], [_h(1, [1], [6, 7, 0])], [_h(1, [6], [3])], [_h(2, [1], [6, 7])]],
-    2: [[_h(0, [2], [4, 1, 3])], [_h(0, [0], [5])], [_h(1, [2], [4, 1, 3])], [_h(2, [2], [4, 1, 3])]],
-    3: [[_h(0, [3], [5, 4, 0])], [_w(4)], [_h(1, [3], [5, 0])], [_h(2, [3], [5], "lo"), _h(2, [4], [0], "hi")]],
-    4: [[_h(0, [4], [6, 2, 7])], [_w(3, "hi")], [_h(1, [4], [6, 2, 3, 7], "lo")], [_h(1, [3], [7])],
-        [_h(2, [4], [6, 2], "lo"), _h(2, [3], [7], "hi")]],
-    5: [[_h(0, [5], [3, 6, 4])], [_h(0, [3], [7])], [_h(1, [5], [3, 6, 4])], [_h(2, [5], [3, 6])]],
-    6: [[_h(0, [6], [4, 0, 1, 5, 7])], [_h(0, [4], [0])], [_h(1, [6], [1, 0, 4, 5, 7])], [_h(1, [4], [0])],
-        [_h(2, [6], [0, 1, 4, 5, 7])]],
-    7: [[_h(0, [7], [1, 0, 4])], [_w(0)], [_h(1, [7], [1, 4])], [_h(1, [0], [5])], [_h(2, [0], [5])], [_h(2, [7], [1])]],
+    0: [[_h(0, [0], [2, 7])], [_w(0, 7)], [_w(1, 7)], [_h(1, [0], [2])], [_h(1, [7], [3, 2])], [_h(2, [7, 0], [2, 3])]],
+    1: [[_h(0, [1], [6, 7]), _h(0, [1], [0], "on")], [_h(0, [7], [2, 3]), _h(0, [7], [0], "on")],
+        [_h(1, [1], [6, 7]), _h(1, [1], [0], "on")], [_h(1, [6], [3])], [_h(2, [1], [6, 7])]],
+    2: [[_h(0, [2], [4, 1]), _h(0, [2], [3], "on")], [_h(0, [0], [5])], [_h(1, [2], [4, 1]), _h(1, [2], [3], "on")],
+        [_h(2, [2], [4, 1]), _h(2, [2], [3], "on")]],
+    3: [[_h(0, [3], [4, 5, 0])], [_w(0, 4)], [_w(1, 4)], [_h(1, [3], [0, 5])], [_h(2, [3], [5], "lo"), _h(2, [4], [0], "hi")]],
+    4: [[_h(0, [4], [6, 2])], [_w(0, 3)], [_w(1, 3)], [_h(1, [4], [6, 7, 2, 3])], [_h(1, [3], [7])], [_h(2, [4], [6, 2])],
+        [_h(2, [3], [7])]],
+    5: [[_h(0, [5], [6, 3]), _h(0, [5], [4], "on")], [_h(0, [3], [7])], [_h(1, [5], [6, 3]), _h(1, [5], [4], "on")],
+        [_h(2, [5], [3, 6])]],
+    6: [[_h(0, [6], [4, 0, 1, 5]), _h(0, [6], [7], "on")], [_h(0, [4], [0]), _h(0, [4], [7], "on")],
+        [_h(1, [6], [1, 0, 4, 5]), _h(1, [6], [7], "on")], [_h(1, [4], [0])], [_h(2, [6], [0, 1, 4, 5]), _h(2, [6], [7], "on")]],
+    7: [[_h(0, [7], [1, 4])], [_w(0, 0)], [_w(1, 0)], [_h(1, [7], [1, 4])], [_h(1, [0], [5])], [_h(2, [0], [5])],
+        [_h(2, [7], [1])]],
 }
 
 GROUPS = {
-    0: [(1, 0, [0, 6, 7, 4]), (1, 7, [1, 3, 6, 7]), (2, 0, [0, 6, 4, 7]), (2, 7, [7, 1, 6, 3]), (3, 0, [0, 7, 6, 4])],
-    1: [(1, 1, [1, 2, 6, 7]), (2, 1, [1, 6, 2, 7]), (3, 1, [1, 2, 7, 6])],
+    0: [(1, 0, [0, 6, 7, 4]), (1, 7, [1, 3, 6, 7]), (2, 7, [7, 6, 1, 3]), (2, 0, [0, 7, 6, 4]), (3, 0, [7, 0, 6, 4])],
+    1: [(1, 1, [1, 7, 2, 6]), (2, 1, [1, 6, 2, 7]), (3, 1, [1, 6, 7, 2])],
     2: [(1, 2, [2, 0, 4, 7]), (2, 2, [2, 4, 0, 7]), (3, 2, [2, 4, 0, 7])],
-    3: [(1, 3, [3, 2, 5, 7]), (2, 3, [3, 2, 5, 7]), (2, 4, [3, 2, 4, 6]), (3, 3, [3, 2, 5, 7])],
-    4: [(1, 4, [4, 2, 3, 6]), (1, 3, [2, 3, 5, 7]), (2, 4, [4, 6, 3, 2]), (2, 3, [3, 2, 5, 7]), (3, 4, [4, 3, 2, 6])],
-    5: [(1, 5, [5, 3, 6, 0]), (2, 5, [5, 6, 3, 0]), (3, 5, [5, 0, 3, 6])],
-    6: [(1, 6, [6, 1, 4, 5]), (2, 6, [6, 1, 4, 5]), (3, 6, [6, 1, 4, 5])],
-    7: [(1, 7, [7, 6, 1, 3]), (1, 0, [7, 6, 0, 4]), (2, 0, [7, 0, 4, 6]), (2, 7, [7, 1, 6, 3]), (3, 7, [7, 1, 6, 3])],
+    3: [(1, 3, [3, 2, 5, 7]), (2, 3, [3, 2, 5, 7]), (2, 4, [3, 2, 4, 6]), (3, 3, [3, 5, 2, 7])],
+    4: [(1, 4, [4, 3, 2, 6]), (1, 3, [2, 3, 5, 7]), (2, 4, [4, 3, 6, 2]), (2, 3, [3, 2, 5, 7]), (3, 4, [4, 3, 6, 2])],
+    5: [(1, 5, [5, 3, 0, 6]), (2, 5, [5, 6, 3, 0]), (3, 5, [0, 5, 6, 3])],
+    6: [(1, 6, [6, 4, 1, 5]), (2, 6, [6, 4, 1, 5]), (3, 6, [6, 4, 1, 5])],
+    7: [(1, 7, [7, 6, 1, 3]), (1, 0, [0, 4, 6, 7]), (2, 0, [6, 7, 0, 4]), (2, 7, [6, 7, 1, 3]), (3, 7, [7, 6, 3, 1])],
 }
 
 
@@ -86,31 +92,25 @@ def _plan(cores, topo):
                 off = topo.mask(me, c)
         calls[r] = []
         for call in SENDS[r]:
-            now, later = [], []
+            now = []
             for kind, t, js, dests, part in call:
                 for d in dests:
                     assert topo.may_write(me, cores[d])
-                far = [d for d in dests if not near(me, cores[d])]
-                nbr = [d for d in dests if near(me, cores[d])]
-                for group in (far, nbr):
-                    if not group:
-                        continue
-                    m = topo.mask(me, cores[group[0]])
-                    eng = _bits(m & off) if group is far else _bits(m & ~off)
-                    if part == "lo":
-                        eng = eng[:len(eng) // 2]
-                    elif part == "hi":
-                        eng = eng[len(eng) // 2:]
-                    (later if (group is nbr and t == 0 and far) else now).append((kind, t, js, group, eng))
-                    for d in group:
-                        if kind == "w":
-                            wcount[d] = len(eng)
-                        for j in js:
-                            assert (d, (t, j)) not in have
-                            have[(d, (t, j))] = ("s%d%d" % (t, js[0]), len(eng))
+                    assert near(me, cores[d]) or part != "on"
+                m = topo.mask(me, cores[dests[0]])
+                eng = _bits(m & ~off) if part == "on" else _bits(m & off)
+                if part == "lo":
+                    eng = eng[:len(eng) // 2]
+                elif part == "hi":
+                    eng = eng[len(eng) // 2:]
+                now.append((kind, t, js, dests, eng))
+                for d in dests:
+                    if kind == "w":
+                        wcount[d] = len(eng)
+                    for j in js:
+                        assert (d, (t, j)) not in have
+                        have[(d, (t, j))] = ("s%d%d" % (t, js[0]), len(eng))
             calls[r].append(now)
-            if later:
-                calls[r].append(later)
     return have, calls, wcount
 
 
@@ -128,20 +128,22 @@ def rank_program(g, core, T, topo):
         c0 = _col(t, js[0])
         return T.h[:, c0:c0 + TK * len(js)]
 
+    g.sync.dma_start(T.xd[:], T.x[:]).then_inc(S.sxd, 16)
     g.sync.dma_start(hs(0, [r]), T.x[:]).then_inc(S["s0%d" % r], 16)
-    g.scalar.dma_start(T.wo[:], T.w[:]).then_inc(S.sw, 16)
+    for hf in range(2):
+        g.scalar.dma_start(T.wo[:, HW * hf:HW * hf + HW], T.w[:, HW * hf:HW * hf + HW]).then_inc(S["sw%d" % hf], 16)
     g.vector.memset(T.zero[:], 0.0).then_inc(S.sz, 1)
     g.vector.wait_ge(S.sz, 1)
 
     seen = set()
     for gi, (t, k, order) in enumerate(GROUPS[r]):
         assert sorted(order) == sorted(mask_table[k]) and (k == r or REP[r] == k)
-        wt, wsem = (T.wo, ("sw", 16)) if k == r else (T.wr, ("swr", wcount[r]))
+        wt, wname, wn = (T.wo, "sw%d", 16) if k == r else (T.wr, "swr%d", wcount[r])
         ps = T["p%d" % gi]
         mm = None
         for n, j in enumerate(order):
             i = mask_table[k].index(j)
-            for sem in (wsem, have[(r, (t - 1, j))]):
+            for sem in ((wname % (P * i // HW), wn), have[(r, (t - 1, j))]):
                 if sem not in seen:
                     g.tensor.wait_ge(S[sem[0]], sem[1])
                     seen.add(sem)
@@ -155,7 +157,8 @@ def rank_program(g, core, T, topo):
     for call in calls[r]:
         transfers = []
         for kind, t, js, dests, eng in call:
-            for sem in ([("sw", 16)] if kind == "w" else [have[(r, (t, j))] for j in js]):
+            mine = kind == "h" and t == 0 and js == [r]
+            for sem in ([("sw%d" % t, 16)] if kind == "w" else [("sxd", 16)] if mine else [have[(r, (t, j))] for j in js]):
                 if sem not in seen:
                     g.wait_ge(S[sem[0]], sem[1])
                     seen.add(sem)
@@ -163,7 +166,10 @@ def rank_program(g, core, T, topo):
             for d in dests:
                 rid, pid = topo.addr(T.cores[d], core)
                 ids.append(DstId(rid=rid, pnc=pid))
-            src, dst, rsem = (T.wo[:], T.wr[:], S.swr) if kind == "w" else (hs(t, js), hs(t, js), S["s%d%d" % (t, js[0])])
+            if kind == "w":
+                src, dst, rsem = T.wo[:, HW * t:HW * t + HW], T.wr[:, HW * t:HW * t + HW], S["swr%d" % t]
+            else:
+                src, dst, rsem = (T.xd[:] if mine else hs(t, js)), hs(t, js), S["s%d%d" % (t, js[0])]
             transfers.append(RemoteDMATransfer(dst_ids=ids, dma_engine_mask=_mask(eng), remote_sem=rsem,
                                                srcs=[src], dsts=[dst for _ in dests]))
             total += len(eng)

@@ -2,6 +2,7 @@ from concourse.bass import DstId, RemoteDMATransfer
 from concourse.mybir import AluOpType
 
 N, DEG, TK, TIMES, P = 8, 4, 64, 3, 128
+WORLD = 512
 HW = DEG * P // 2
 ORDER = [1, 2, 3, 4, 5, 6, 7, 0]
 
@@ -10,6 +11,9 @@ SCRATCH = {
     "wo": ("sbuf", [P, DEG * P], "bfloat16"),
     "wr": ("sbuf", [P, DEG * P], "bfloat16"),
     "xd": ("dram", [P, TK], "bfloat16"),
+    "sp": ("sbuf", [P, TK], "bfloat16"),
+    "sr": ("sbuf", [P, TK], "bfloat16"),
+    "tz": ("sbuf", [P, TK], "float32"),
     "zero": ("sbuf", [P, TK], "float32"),
     "yb": ("sbuf", [P, TK], "bfloat16"),
     "p0": ("psum", [P, 512], "float32"),
@@ -17,11 +21,13 @@ SCRATCH = {
     "p2": ("psum", [P, 512], "float32"),
     "p3": ("psum", [P, 512], "float32"),
     "p4": ("psum", [P, 512], "float32"),
+    "p5": ("psum", [P, 512], "float32"),
 }
-SEMAPHORES = (["s%d%d" % (t, j) for t in range(TIMES) for j in range(N)]
-              + ["m%d" % i for i in range(5)] + ["sw0", "sw1", "swr0", "swr1", "sxd", "sz", "s3", "sy", "sent"])
+SEMAPHORES = (["s%d%d" % (t, j) for t in range(TIMES) for j in range(N)] + ["m%d" % i for i in range(6)]
+              + ["sw0", "sw1", "swr0", "swr1", "swv", "sxd", "sz", "s3", "sy", "sent", "ssp", "ssr", "sa"])
 
 REP = {0: 7, 7: 0, 4: 3, 3: 4}
+FIRST = {3: 1}
 
 
 def _h(t, js, dests, part="all"):
@@ -32,32 +38,45 @@ def _w(half, dest, part="all"):
     return ("w", half, [], [dest], part)
 
 
+def _v(half):
+    return ("v", half, [], [], "on")
+
+
+def _s(dest, part="all"):
+    return ("s", 0, [], [dest], part)
+
+
 SENDS = {
-    0: [[_h(0, [0], [2, 7])], [_w(0, 7)], [_w(1, 7)], [_h(1, [0], [2])], [_h(1, [7], [3, 2])], [_h(2, [7, 0], [2, 3])]],
-    1: [[_h(0, [1], [6, 7]), _h(0, [1], [0], "on")], [_h(0, [7], [2, 3]), _h(0, [7], [0], "on")],
+    0: [[_h(0, [0], [2])], [_w(0, 7)], [_v(1)], [_s(7)], [_h(1, [0], [2])], [_h(1, [7], [3, 2])],
+        [_h(2, [7, 0], [2, 3])]],
+    1: [[_h(0, [1], [6, 7])], [_h(0, [7], [2, 3])],
         [_h(1, [1], [6, 7]), _h(1, [1], [0], "on")], [_h(1, [6], [3])], [_h(2, [1], [6, 7])]],
     2: [[_h(0, [2], [4, 1]), _h(0, [2], [3], "on")], [_h(0, [0], [5])], [_h(1, [2], [4, 1]), _h(1, [2], [3], "on")],
         [_h(2, [2], [4, 1]), _h(2, [2], [3], "on")]],
-    3: [[_h(0, [3], [4, 5, 0])], [_w(0, 4)], [_w(1, 4)], [_h(1, [3], [0, 5])], [_h(2, [3], [5], "lo"), _h(2, [4], [0], "hi")]],
-    4: [[_h(0, [4], [6, 2])], [_w(0, 3)], [_w(1, 3)], [_h(1, [4], [6, 7, 2, 3])], [_h(1, [3], [7])], [_h(2, [4], [6, 2])],
+    3: [[_h(0, [3], [4, 5, 0])], [_w(1, 4)], [_v(0)], [_s(4)], [_h(1, [3], [0, 5])],
+        [_h(2, [3], [5], "lo"), _h(2, [4], [0], "hi")]],
+    4: [[_h(0, [4], [6, 2])], [_w(0, 3)], [_v(1)], [_h(1, [4], [6, 7, 2, 3])], [_h(1, [3], [7])], [_h(2, [4], [6, 2])],
         [_h(2, [3], [7])]],
-    5: [[_h(0, [5], [6, 3]), _h(0, [5], [4], "on")], [_h(0, [3], [7])], [_h(1, [5], [6, 3]), _h(1, [5], [4], "on")],
-        [_h(2, [5], [3, 6])]],
+    5: [[_h(0, [5], [6, 3])], [_h(0, [3], [7])], [_h(1, [5], [6, 3, 4])], [_h(2, [5], [3, 6])]],
     6: [[_h(0, [6], [4, 0, 1, 5]), _h(0, [6], [7], "on")], [_h(0, [4], [0]), _h(0, [4], [7], "on")],
         [_h(1, [6], [1, 0, 4, 5]), _h(1, [6], [7], "on")], [_h(1, [4], [0])], [_h(2, [6], [0, 1, 4, 5]), _h(2, [6], [7], "on")]],
-    7: [[_h(0, [7], [1, 4])], [_w(0, 0)], [_w(1, 0)], [_h(1, [7], [1, 4])], [_h(1, [0], [5])], [_h(2, [0], [5])],
+    7: [[_h(0, [7], [1, 0, 4])], [_w(0, 0)], [_v(1)], [_s(0)], [_h(1, [7], [1, 4])], [_h(1, [0], [5])], [_h(2, [0], [5])],
         [_h(2, [7], [1])]],
 }
 
 GROUPS = {
-    0: [(1, 0, [0, 6, 7, 4]), (1, 7, [1, 3, 6, 7]), (2, 7, [7, 6, 1, 3]), (2, 0, [0, 7, 6, 4]), (3, 0, [7, 0, 6, 4])],
-    1: [(1, 1, [1, 7, 2, 6]), (2, 1, [1, 6, 2, 7]), (3, 1, [1, 6, 7, 2])],
-    2: [(1, 2, [2, 0, 4, 7]), (2, 2, [2, 4, 0, 7]), (3, 2, [2, 4, 0, 7])],
-    3: [(1, 3, [3, 2, 5, 7]), (2, 3, [3, 2, 5, 7]), (2, 4, [3, 2, 4, 6]), (3, 3, [3, 5, 2, 7])],
-    4: [(1, 4, [4, 3, 2, 6]), (1, 3, [2, 3, 5, 7]), (2, 4, [4, 3, 6, 2]), (2, 3, [3, 2, 5, 7]), (3, 4, [4, 3, 6, 2])],
-    5: [(1, 5, [5, 3, 0, 6]), (2, 5, [5, 6, 3, 0]), (3, 5, [0, 5, 6, 3])],
-    6: [(1, 6, [6, 4, 1, 5]), (2, 6, [6, 4, 1, 5]), (3, 6, [6, 4, 1, 5])],
-    7: [(1, 7, [7, 6, 1, 3]), (1, 0, [0, 4, 6, 7]), (2, 0, [6, 7, 0, 4]), (2, 7, [6, 7, 1, 3]), (3, 7, [7, 6, 3, 1])],
+    0: [(1, 0, [0, 6, 7], "part"), (1, 0, [0, 6, 7, 4], "full"), (1, 7, [3], "fin"), (2, 7, [7, 6, 1, 3], "full"),
+        (2, 0, [0, 7, 6, 4], "full"), (3, 0, [7, 0, 6, 4], "full")],
+    1: [(1, 1, [1, 7, 2, 6], "full"), (2, 1, [1, 6, 2, 7], "full"), (3, 1, [1, 6, 7, 2], "full")],
+    2: [(1, 2, [2, 0, 4, 7], "full"), (2, 2, [2, 4, 0, 7], "full"), (3, 2, [2, 4, 0, 7], "full")],
+    3: [(1, 3, [3, 2, 5], "part"), (1, 3, [3, 2, 5, 7], "full"), (2, 3, [3, 2, 5, 7], "full"), (2, 4, [3, 2, 4, 6], "full"),
+        (3, 3, [3, 5, 2, 7], "full")],
+    4: [(1, 4, [4, 3, 2, 6], "full"), (1, 3, [7], "fin"), (2, 4, [4, 3, 6, 2], "full"), (2, 3, [3, 2, 5, 7], "full"),
+        (3, 4, [4, 3, 6, 2], "full")],
+    5: [(1, 5, [5, 3, 0, 6], "full"), (2, 5, [5, 6, 3, 0], "full"), (3, 5, [0, 5, 6, 3], "full")],
+    6: [(1, 6, [6, 4, 1, 5], "full"), (2, 6, [6, 4, 1, 5], "full"), (3, 6, [6, 4, 1, 5], "full")],
+    7: [(1, 7, [7, 6, 1], "part"), (1, 7, [7, 6, 1, 3], "full"), (1, 0, [4], "fin"), (2, 0, [6, 7, 0, 4], "full"),
+        (2, 7, [6, 7, 1, 3], "full"), (3, 7, [7, 6, 3, 1], "full")],
 }
 
 
@@ -73,22 +92,27 @@ def _mask(engines):
     return sum(1 << b for b in engines)
 
 
+def _near(topo, a, b):
+    return topo.host(a) == topo.host(b) and topo.chip(a) == topo.chip(b)
+
+
+def _helper(me, cores, topo):
+    return [c for c in range(WORLD) if c not in cores and _near(topo, me, c) and topo.die(c) == topo.die(me)][-1]
+
+
 def _plan(cores, topo):
-    have, calls, wcount = {}, {}, {}
+    have, calls, wcount, scount = {}, {}, {}, {}
     for r in range(N):
         have[(r, (0, r))] = ("s0%d" % r, 16)
-        for t, k, _ in GROUPS[r]:
-            if t < TIMES:
+        for t, k, _, mode in GROUPS[r]:
+            if t < TIMES and mode != "part":
                 have[(r, (t, k))] = ("s%d%d" % (t, k), 1)
-
-    def near(a, b):
-        return topo.host(a) == topo.host(b) and topo.chip(a) == topo.chip(b)
 
     for r in range(N):
         me = cores[r]
         off = 0
         for c in cores:
-            if not near(me, c) and topo.may_write(me, c):
+            if not _near(topo, me, c) and topo.may_write(me, c):
                 off = topo.mask(me, c)
         calls[r] = []
         for call in SENDS[r]:
@@ -96,8 +120,8 @@ def _plan(cores, topo):
             for kind, t, js, dests, part in call:
                 for d in dests:
                     assert topo.may_write(me, cores[d])
-                    assert near(me, cores[d]) or part != "on"
-                m = topo.mask(me, cores[dests[0]])
+                    assert _near(topo, me, cores[d]) or part != "on"
+                m = topo.mask(me, _helper(me, cores, topo) if kind == "v" else cores[dests[0]])
                 eng = _bits(m & ~off) if part == "on" else _bits(m & off)
                 if part == "lo":
                     eng = eng[:len(eng) // 2]
@@ -107,19 +131,38 @@ def _plan(cores, topo):
                 for d in dests:
                     if kind == "w":
                         wcount[d] = len(eng)
+                    if kind == "s":
+                        scount[d] = len(eng)
                     for j in js:
                         assert (d, (t, j)) not in have
                         have[(d, (t, j))] = ("s%d%d" % (t, js[0]), len(eng))
             calls[r].append(now)
-    return have, calls, wcount
+    return have, calls, wcount, scount
+
+
+def _helper_program(g, core, T, topo):
+    S = T.sem
+    for d, o in REP.items():
+        own = T.cores[o]
+        if _near(topo, own, core) and _helper(own, T.cores, topo) == core:
+            hf = 1 - FIRST.get(o, 0)
+            arrive = len(_bits(topo.mask(own, core) & ~topo.mask(own, T.cores[d])))
+            eng = topo.mask(core, T.cores[d])
+            rid, pid = topo.addr(T.cores[d], core)
+            g.wait_ge(S.swv, arrive)
+            piece = T.wr[:, HW * hf:HW * hf + HW]
+            g.remote_dma_fused([RemoteDMATransfer(dst_ids=[DstId(rid=rid, pnc=pid)], dma_engine_mask=eng,
+                                                  remote_sem=S["swr%d" % hf], srcs=[piece], dsts=[piece])], local_sem=S.sent)
+            g.wait_ge(S.sent, len(_bits(eng)))
 
 
 def rank_program(g, core, T, topo):
     r = T.rank_of(core)
     if r is None:
+        _helper_program(g, core, T, topo)
         return
     mask_table = T.tables["MASK"]
-    have, calls, wcount = _plan(T.cores, topo)
+    have, calls, wcount, scount = _plan(T.cores, topo)
     S = T.sem
 
     def hs(t, js):
@@ -130,14 +173,16 @@ def rank_program(g, core, T, topo):
 
     g.sync.dma_start(T.xd[:], T.x[:]).then_inc(S.sxd, 16)
     g.sync.dma_start(hs(0, [r]), T.x[:]).then_inc(S["s0%d" % r], 16)
-    for hf in range(2):
+    f = FIRST.get(r, 0)
+    for hf in (f, 1 - f):
         g.scalar.dma_start(T.wo[:, HW * hf:HW * hf + HW], T.w[:, HW * hf:HW * hf + HW]).then_inc(S["sw%d" % hf], 16)
     g.vector.memset(T.zero[:], 0.0).then_inc(S.sz, 1)
     g.vector.wait_ge(S.sz, 1)
 
     seen = set()
-    for gi, (t, k, order) in enumerate(GROUPS[r]):
-        assert sorted(order) == sorted(mask_table[k]) and (k == r or REP[r] == k)
+    for gi, (t, k, order, mode) in enumerate(GROUPS[r]):
+        assert k == r or REP[r] == k
+        assert set(order) <= set(mask_table[k]) and (mode != "full" or len(order) == DEG)
         wt, wname, wn = (T.wo, "sw%d", 16) if k == r else (T.wr, "swr%d", wcount[r])
         ps = T["p%d" % gi]
         mm = None
@@ -147,31 +192,46 @@ def rank_program(g, core, T, topo):
                 if sem not in seen:
                     g.tensor.wait_ge(S[sem[0]], sem[1])
                     seen.add(sem)
-            mm = g.tensor.matmul(ps[:, 0:TK], wt[:, P * i:P * i + P], hs(t - 1, [j]), start=(n == 0), stop=(n == DEG - 1))
+            mm = g.tensor.matmul(ps[:, 0:TK], wt[:, P * i:P * i + P], hs(t - 1, [j]), start=(n == 0),
+                                 stop=(n == len(order) - 1))
         mm.then_inc(S["m%d" % gi], 1)
         g.vector.wait_ge(S["m%d" % gi], 1)
+        if mode == "part":
+            g.vector.tensor_copy(T.sp[:], ps[:, 0:TK]).then_inc(S.ssp, 1)
+            continue
         out, osem = (hs(t, [k]), S["s%d%d" % (t, k)]) if t < TIMES else (T.yb[:], S.s3)
-        g.vector.tensor_tensor(out, ps[:, 0:TK], T.zero[:], AluOpType.max).then_inc(osem, 1)
+        if mode == "fin":
+            g.vector.wait_ge(S.ssr, scount[r])
+            g.vector.tensor_tensor(T.tz[:], ps[:, 0:TK], T.sr[:], AluOpType.add).then_inc(S.sa, 1)
+            g.vector.wait_ge(S.sa, 1)
+            g.vector.tensor_tensor(out, T.tz[:], T.zero[:], AluOpType.max).then_inc(osem, 1)
+        else:
+            g.vector.tensor_tensor(out, ps[:, 0:TK], T.zero[:], AluOpType.max).then_inc(osem, 1)
 
     seen, total = set(), 0
     for call in calls[r]:
         transfers = []
         for kind, t, js, dests, eng in call:
             mine = kind == "h" and t == 0 and js == [r]
-            for sem in ([("sw%d" % t, 16)] if kind == "w" else [("sxd", 16)] if mine else [have[(r, (t, j))] for j in js]):
+            for sem in ([("sw%d" % t, 16)] if kind in ("w", "v") else [("ssp", 1)] if kind == "s" else
+                        [("sxd", 16)] if mine else [have[(r, (t, j))] for j in js]):
                 if sem not in seen:
                     g.wait_ge(S[sem[0]], sem[1])
                     seen.add(sem)
+            targets = [_helper(core, T.cores, topo)] if kind == "v" else [T.cores[d] for d in dests]
             ids = []
-            for d in dests:
-                rid, pid = topo.addr(T.cores[d], core)
+            for c in targets:
+                rid, pid = topo.addr(c, core)
                 ids.append(DstId(rid=rid, pnc=pid))
-            if kind == "w":
-                src, dst, rsem = T.wo[:, HW * t:HW * t + HW], T.wr[:, HW * t:HW * t + HW], S["swr%d" % t]
+            if kind in ("w", "v"):
+                src, dst = T.wo[:, HW * t:HW * t + HW], T.wr[:, HW * t:HW * t + HW]
+                rsem = S["swr%d" % t] if kind == "w" else S.swv
+            elif kind == "s":
+                src, dst, rsem = T.sp[:], T.sr[:], S.ssr
             else:
                 src, dst, rsem = (T.xd[:] if mine else hs(t, js)), hs(t, js), S["s%d%d" % (t, js[0])]
             transfers.append(RemoteDMATransfer(dst_ids=ids, dma_engine_mask=_mask(eng), remote_sem=rsem,
-                                               srcs=[src], dsts=[dst for _ in dests]))
+                                               srcs=[src], dsts=[dst for _ in targets]))
             total += len(eng)
         g.remote_dma_fused(transfers, local_sem=S.sent)
     g.wait_ge(S.sent, total)

from concourse.bass import DstId, RemoteDMATransfer
from concourse.mybir import AluOpType

N, DEG, TK, TIMES, P = 8, 4, 64, 3, 128
WORLD = 512
HW = DEG * P // 2
ORDER = [1, 2, 3, 4, 5, 6, 7, 0]

SCRATCH = {
    "h": ("sbuf", [P, TIMES * N * TK], "bfloat16"),
    "wo": ("sbuf", [P, DEG * P], "bfloat16"),
    "wr": ("sbuf", [P, DEG * P], "bfloat16"),
    "xd": ("dram", [P, TK], "bfloat16"),
    "sp": ("sbuf", [P, TK], "bfloat16"),
    "sr": ("sbuf", [P, TK], "bfloat16"),
    "tz": ("sbuf", [P, TK], "float32"),
    "zero": ("sbuf", [P, TK], "float32"),
    "yb": ("sbuf", [P, TK], "bfloat16"),
    "p0": ("psum", [P, 512], "float32"),
    "p1": ("psum", [P, 512], "float32"),
    "p2": ("psum", [P, 512], "float32"),
    "p3": ("psum", [P, 512], "float32"),
    "p4": ("psum", [P, 512], "float32"),
    "p5": ("psum", [P, 512], "float32"),
}
SEMAPHORES = (["s%d%d" % (t, j) for t in range(TIMES) for j in range(N)] + ["m%d" % i for i in range(6)]
              + ["sw0", "sw1", "swr0", "swr1", "swv", "sxd", "sz", "s3", "sy", "sent", "ssp", "ssr", "sa"])

REP = {0: 7, 7: 0, 4: 3, 3: 4}
FIRST = {3: 1}


def _h(t, js, dests, part="all"):
    return ("h", t, js, dests, part)


def _w(half, dest, part="all"):
    return ("w", half, [], [dest], part)


def _v(half):
    return ("v", half, [], [], "on")


def _s(dest, part="all"):
    return ("s", 0, [], [dest], part)


SENDS = {
    0: [[_h(0, [0], [2])], [_w(0, 7)], [_v(1)], [_s(7)], [_h(1, [0], [2])], [_h(1, [7], [3, 2])],
        [_h(2, [7, 0], [2, 3])]],
    1: [[_h(0, [1], [6, 7])], [_h(0, [7], [2, 3])],
        [_h(1, [1], [6, 7]), _h(1, [1], [0], "on")], [_h(1, [6], [3])], [_h(2, [1], [6, 7])]],
    2: [[_h(0, [2], [4, 1]), _h(0, [2], [3], "on")], [_h(0, [0], [5])], [_h(1, [2], [4, 1]), _h(1, [2], [3], "on")],
        [_h(2, [2], [4, 1]), _h(2, [2], [3], "on")]],
    3: [[_h(0, [3], [4, 5, 0])], [_w(1, 4)], [_v(0)], [_s(4)], [_h(1, [3], [0, 5])],
        [_h(2, [3], [5], "lo"), _h(2, [4], [0], "hi")]],
    4: [[_h(0, [4], [6, 2])], [_w(0, 3)], [_v(1)], [_h(1, [4], [6, 7, 2, 3])], [_h(1, [3], [7])], [_h(2, [4], [6, 2])],
        [_h(2, [3], [7])]],
    5: [[_h(0, [5], [6, 3])], [_h(0, [3], [7])], [_h(1, [5], [6, 3, 4])], [_h(2, [5], [3, 6])]],
    6: [[_h(0, [6], [4, 0, 1, 5]), _h(0, [6], [7], "on")], [_h(0, [4], [0]), _h(0, [4], [7], "on")],
        [_h(1, [6], [1, 0, 4, 5]), _h(1, [6], [7], "on")], [_h(1, [4], [0])], [_h(2, [6], [0, 1, 4, 5]), _h(2, [6], [7], "on")]],
    7: [[_h(0, [7], [1, 0, 4])], [_w(0, 0)], [_v(1)], [_s(0)], [_h(1, [7], [1, 4])], [_h(1, [0], [5])], [_h(2, [0], [5])],
        [_h(2, [7], [1])]],
}

GROUPS = {
    0: [(1, 0, [0, 6, 7], "part"), (1, 0, [0, 6, 7, 4], "full"), (1, 7, [3], "fin"), (2, 7, [7, 6, 1, 3], "full"),
        (2, 0, [0, 7, 6, 4], "full"), (3, 0, [7, 0, 6, 4], "full")],
    1: [(1, 1, [1, 7, 2, 6], "full"), (2, 1, [1, 6, 2, 7], "full"), (3, 1, [1, 6, 7, 2], "full")],
    2: [(1, 2, [2, 0, 4, 7], "full"), (2, 2, [2, 4, 0, 7], "full"), (3, 2, [2, 4, 0, 7], "full")],
    3: [(1, 3, [3, 2, 5], "part"), (1, 3, [3, 2, 5, 7], "full"), (2, 3, [3, 2, 5, 7], "full"), (2, 4, [3, 2, 4, 6], "full"),
        (3, 3, [3, 5, 2, 7], "full")],
    4: [(1, 4, [4, 3, 2, 6], "full"), (1, 3, [7], "fin"), (2, 4, [4, 3, 6, 2], "full"), (2, 3, [3, 2, 5, 7], "full"),
        (3, 4, [4, 3, 6, 2], "full")],
    5: [(1, 5, [5, 3, 0, 6], "full"), (2, 5, [5, 6, 3, 0], "full"), (3, 5, [0, 5, 6, 3], "full")],
    6: [(1, 6, [6, 4, 1, 5], "full"), (2, 6, [6, 4, 1, 5], "full"), (3, 6, [6, 4, 1, 5], "full")],
    7: [(1, 7, [7, 6, 1], "part"), (1, 7, [7, 6, 1, 3], "full"), (1, 0, [4], "fin"), (2, 0, [6, 7, 0, 4], "full"),
        (2, 7, [6, 7, 1, 3], "full"), (3, 7, [7, 6, 3, 1], "full")],
}


def _col(t, j):
    return (t * N + ORDER.index(j)) * TK


def _bits(m):
    return [b for b in range(m.bit_length()) if (m >> b) & 1]


def _mask(engines):
    return sum(1 << b for b in engines)


def _near(topo, a, b):
    return topo.host(a) == topo.host(b) and topo.chip(a) == topo.chip(b)


def _helper(me, cores, topo):
    return [c for c in range(WORLD) if c not in cores and _near(topo, me, c) and topo.die(c) == topo.die(me)][-1]


def _plan(cores, topo):
    have, calls, wcount, scount = {}, {}, {}, {}
    for r in range(N):
        have[(r, (0, r))] = ("s0%d" % r, 16)
        for t, k, _, mode in GROUPS[r]:
            if t < TIMES and mode != "part":
                have[(r, (t, k))] = ("s%d%d" % (t, k), 1)

    for r in range(N):
        me = cores[r]
        off = 0
        for c in cores:
            if not _near(topo, me, c) and topo.may_write(me, c):
                off = topo.mask(me, c)
        calls[r] = []
        for call in SENDS[r]:
            now = []
            for kind, t, js, dests, part in call:
                for d in dests:
                    assert topo.may_write(me, cores[d])
                    assert _near(topo, me, cores[d]) or part != "on"
                m = topo.mask(me, _helper(me, cores, topo) if kind == "v" else cores[dests[0]])
                eng = _bits(m & ~off) if part == "on" else _bits(m & off)
                if part == "lo":
                    eng = eng[:len(eng) // 2]
                elif part == "hi":
                    eng = eng[len(eng) // 2:]
                now.append((kind, t, js, dests, eng))
                for d in dests:
                    if kind == "w":
                        wcount[d] = len(eng)
                    if kind == "s":
                        scount[d] = len(eng)
                    for j in js:
                        assert (d, (t, j)) not in have
                        have[(d, (t, j))] = ("s%d%d" % (t, js[0]), len(eng))
            calls[r].append(now)
    return have, calls, wcount, scount


def _helper_program(g, core, T, topo):
    S = T.sem
    for d, o in REP.items():
        own = T.cores[o]
        if _near(topo, own, core) and _helper(own, T.cores, topo) == core:
            hf = 1 - FIRST.get(o, 0)
            arrive = len(_bits(topo.mask(own, core) & ~topo.mask(own, T.cores[d])))
            eng = topo.mask(core, T.cores[d])
            rid, pid = topo.addr(T.cores[d], core)
            g.wait_ge(S.swv, arrive)
            piece = T.wr[:, HW * hf:HW * hf + HW]
            g.remote_dma_fused([RemoteDMATransfer(dst_ids=[DstId(rid=rid, pnc=pid)], dma_engine_mask=eng,
                                                  remote_sem=S["swr%d" % hf], srcs=[piece], dsts=[piece])], local_sem=S.sent)
            g.wait_ge(S.sent, len(_bits(eng)))


def rank_program(g, core, T, topo):
    r = T.rank_of(core)
    if r is None:
        _helper_program(g, core, T, topo)
        return
    mask_table = T.tables["MASK"]
    have, calls, wcount, scount = _plan(T.cores, topo)
    S = T.sem

    def hs(t, js):
        for a, b in zip(js, js[1:]):
            assert ORDER.index(b) == ORDER.index(a) + 1
        c0 = _col(t, js[0])
        return T.h[:, c0:c0 + TK * len(js)]

    g.sync.dma_start(T.xd[:], T.x[:]).then_inc(S.sxd, 16)
    g.sync.dma_start(hs(0, [r]), T.x[:]).then_inc(S["s0%d" % r], 16)
    f = FIRST.get(r, 0)
    for hf in (f, 1 - f):
        g.scalar.dma_start(T.wo[:, HW * hf:HW * hf + HW], T.w[:, HW * hf:HW * hf + HW]).then_inc(S["sw%d" % hf], 16)
    g.vector.memset(T.zero[:], 0.0).then_inc(S.sz, 1)
    g.vector.wait_ge(S.sz, 1)

    seen = set()
    for gi, (t, k, order, mode) in enumerate(GROUPS[r]):
        assert k == r or REP[r] == k
        assert set(order) <= set(mask_table[k]) and (mode != "full" or len(order) == DEG)
        wt, wname, wn = (T.wo, "sw%d", 16) if k == r else (T.wr, "swr%d", wcount[r])
        ps = T["p%d" % gi]
        mm = None
        for n, j in enumerate(order):
            i = mask_table[k].index(j)
            for sem in ((wname % (P * i // HW), wn), have[(r, (t - 1, j))]):
                if sem not in seen:
                    g.tensor.wait_ge(S[sem[0]], sem[1])
                    seen.add(sem)
            mm = g.tensor.matmul(ps[:, 0:TK], wt[:, P * i:P * i + P], hs(t - 1, [j]), start=(n == 0),
                                 stop=(n == len(order) - 1))
        mm.then_inc(S["m%d" % gi], 1)
        g.vector.wait_ge(S["m%d" % gi], 1)
        if mode == "part":
            g.vector.tensor_copy(T.sp[:], ps[:, 0:TK]).then_inc(S.ssp, 1)
            continue
        out, osem = (hs(t, [k]), S["s%d%d" % (t, k)]) if t < TIMES else (T.yb[:], S.s3)
        if mode == "fin":
            g.vector.wait_ge(S.ssr, scount[r])
            g.vector.tensor_tensor(T.tz[:], ps[:, 0:TK], T.sr[:], AluOpType.add).then_inc(S.sa, 1)
            g.vector.wait_ge(S.sa, 1)
            g.vector.tensor_tensor(out, T.tz[:], T.zero[:], AluOpType.max).then_inc(osem, 1)
        else:
            g.vector.tensor_tensor(out, ps[:, 0:TK], T.zero[:], AluOpType.max).then_inc(osem, 1)

    seen, total = set(), 0
    for call in calls[r]:
        transfers = []
        for kind, t, js, dests, eng in call:
            mine = kind == "h" and t == 0 and js == [r]
            for sem in ([("sw%d" % t, 16)] if kind in ("w", "v") else [("ssp", 1)] if kind == "s" else
                        [("sxd", 16)] if mine else [have[(r, (t, j))] for j in js]):
                if sem not in seen:
                    g.wait_ge(S[sem[0]], sem[1])
                    seen.add(sem)
            targets = [_helper(core, T.cores, topo)] if kind == "v" else [T.cores[d] for d in dests]
            ids = []
            for c in targets:
                rid, pid = topo.addr(c, core)
                ids.append(DstId(rid=rid, pnc=pid))
            if kind in ("w", "v"):
                src, dst = T.wo[:, HW * t:HW * t + HW], T.wr[:, HW * t:HW * t + HW]
                rsem = S["swr%d" % t] if kind == "w" else S.swv
            elif kind == "s":
                src, dst, rsem = T.sp[:], T.sr[:], S.ssr
            else:
                src, dst, rsem = (T.xd[:] if mine else hs(t, js)), hs(t, js), S["s%d%d" % (t, js[0])]
            transfers.append(RemoteDMATransfer(dst_ids=ids, dma_engine_mask=_mask(eng), remote_sem=rsem,
                                               srcs=[src], dsts=[dst for _ in targets]))
            total += len(eng)
        g.remote_dma_fused(transfers, local_sem=S.sent)
    g.wait_ge(S.sent, total)

    g.sync.wait_ge(S.s3, 1)
    g.sync.dma_start(T.y[:], T.yb[:]).then_inc(S.sy, 16)
    g.sync.wait_ge(S.sy, 16)
